import numpy as np
import ml_dtypes

BF16 = ml_dtypes.bfloat16


def bf(x):
    return np.asarray(x, np.float32).astype(BF16)


def f32(x):
    return np.asarray(x, np.float32)


def f64(x):
    return np.asarray(x).astype(np.float64)


def striped(idx):
    return np.tile(idx.reshape(-1, 16).T, (8, 1))


def rows(idx, k):
    return np.tile(idx, (k, 1))


def look(tab, idx):
    return np.take_along_axis(f64(tab), rows(idx, len(tab)), axis=1)


K, S, V, N = 128, 2048, 1024, 1024


def setup_inputs():
    return {"tab": f32(np.random.standard_normal((2, K, S))), "y": f32(np.random.standard_normal((K, V))), "offs": striped(np.random.permutation(S)[:N])}


def reference(tab, y, offs):
    idx = offs[:16].T.reshape(-1)
    x = (look(tab[0], idx) + f64(y)) * (1.0 / (1.0 + np.exp(-look(tab[1], idx))))
    return x

@@ -1,0 +1,34 @@
+import concourse.mybir as mybir
+
+F32 = mybir.dt.float32
+U16 = mybir.dt.uint16
+ENTRIES_PER_COLUMN = 16
+PIECE = 512
+
+
+def tile_lookup_vg_addsig_out_kernel(tc, tab, y, offs, out):
+    nc = tc.nc
+    rows, places = tab.shape[1], tab.shape[2]
+    entries = y.shape[1]
+
+    with tc.tile_pool(name="held", bufs=1) as held:
+        offsets = held.tile([rows, entries // ENTRIES_PER_COLUMN], U16, name="offsets")
+        values = held.tile([rows, places], F32, name="values")
+        gates = held.tile([rows, places], F32, name="gates")
+        stream = held.tile([rows, entries], F32, name="stream")
+
+        nc.sync.dma_start(offsets[:], offs)
+        nc.sync.dma_start(values[:], tab[0])
+        nc.sync.dma_start(stream[:], y)
+        nc.sync.dma_start(gates[:], tab[1])
+
+        for start in range(0, entries, PIECE):
+            stop = start + PIECE
+            listed = offsets[:, start // ENTRIES_PER_COLUMN : stop // ENTRIES_PER_COLUMN]
+            summed = held.tile([rows, PIECE], F32, name=f"summed{start}")
+            opened = held.tile([rows, PIECE], F32, name=f"opened{start}")
+            product = held.tile([rows, PIECE], F32, name=f"product{start}")
+            nc.vector.tensor_tensor(summed[:], values[:].indirect(listed), stream[:, start:stop], mybir.AluOpType.add)
+            nc.scalar.activation(opened[:], gates[:].indirect(listed), mybir.ActivationFunctionType.Sigmoid)
+            nc.vector.tensor_tensor(product[:], summed[:], opened[:], mybir.AluOpType.mult)
+            nc.sync.dma_start(out[:, start:stop], product[:])

@@ -3,32 +3,59 @@ import concourse.mybir as mybir
 F32 = mybir.dt.float32
 U16 = mybir.dt.uint16
 ENTRIES_PER_COLUMN = 16
-PIECE = 512
+PIECE = 256
 
 
 def tile_lookup_vg_addsig_out_kernel(tc, tab, y, offs, out):
     nc = tc.nc
     rows, places = tab.shape[1], tab.shape[2]
     entries = y.shape[1]
+    half = entries // 2
+    pieces = [slice(start, start + PIECE) for start in range(0, entries, PIECE)]
+    early = [piece for piece in pieces if piece.start < half]
+    late = [piece for piece in pieces if piece.start >= half]
 
     with tc.tile_pool(name="held", bufs=1) as held:
         offsets = held.tile([rows, entries // ENTRIES_PER_COLUMN], U16, name="offsets")
         values = held.tile([rows, places], F32, name="values")
         gates = held.tile([rows, places], F32, name="gates")
         stream = held.tile([rows, entries], F32, name="stream")
+        summed = held.tile([rows, entries], F32, name="summed")
+        opened = held.tile([rows, entries], F32, name="opened")
+        product = held.tile([rows, entries], F32, name="product")
+        warm_in = held.tile([rows, 8], F32, name="warm_in")
+        warm_out = held.tile([rows, 8], F32, name="warm_out")
+
+        def listed(piece):
+            return offsets[:, piece.start // ENTRIES_PER_COLUMN : piece.stop // ENTRIES_PER_COLUMN]
+
+        def add_values(piece):
+            nc.vector.tensor_tensor(
+                summed[:, piece], values[:].indirect(listed(piece)), stream[:, piece], mybir.AluOpType.add
+            )
+
+        def multiply_and_store(piece):
+            nc.vector.tensor_tensor(product[:, piece], summed[:, piece], opened[:, piece], mybir.AluOpType.mult)
+            nc.sync.dma_start(out[:, piece], product[:, piece])
 
         nc.sync.dma_start(offsets[:], offs)
         nc.sync.dma_start(values[:], tab[0])
-        nc.sync.dma_start(stream[:], y)
+        nc.sync.dma_start(stream[:, :half], y[:, :half])
         nc.sync.dma_start(gates[:], tab[1])
+        for piece in late:
+            nc.sync.dma_start(stream[:, piece], y[:, piece])
 
-        for start in range(0, entries, PIECE):
-            stop = start + PIECE
-            listed = offsets[:, start // ENTRIES_PER_COLUMN : stop // ENTRIES_PER_COLUMN]
-            summed = held.tile([rows, PIECE], F32, name=f"summed{start}")
-            opened = held.tile([rows, PIECE], F32, name=f"opened{start}")
-            product = held.tile([rows, PIECE], F32, name=f"product{start}")
-            nc.vector.tensor_tensor(summed[:], values[:].indirect(listed), stream[:, start:stop], mybir.AluOpType.add)
-            nc.scalar.activation(opened[:], gates[:].indirect(listed), mybir.ActivationFunctionType.Sigmoid)
-            nc.vector.tensor_tensor(product[:], summed[:], opened[:], mybir.AluOpType.mult)
-            nc.sync.dma_start(out[:, start:stop], product[:])
+        nc.vector.memset(warm_in[:], 0.0)
+        nc.scalar.activation(warm_out[:], warm_in[:], mybir.ActivationFunctionType.Sigmoid)
+
+        for piece in early:
+            add_values(piece)
+        for piece in pieces:
+            nc.scalar.activation(
+                opened[:, piece], gates[:].indirect(listed(piece)), mybir.ActivationFunctionType.Sigmoid
+            )
+        for early_piece, late_piece in zip(early, late):
+            add_values(late_piece)
+            multiply_and_store(early_piece)
+        for piece in late:
+            multiply_and_store(piece)

@@ -10,10 +10,11 @@ def tile_lookup_vg_addsig_out_kernel(tc, tab, y, offs, out):
     nc = tc.nc
     rows, places = tab.shape[1], tab.shape[2]
     entries = y.shape[1]
-    half = entries // 2
-    pieces = [slice(start, start + PIECE) for start in range(0, entries, PIECE)]
-    early = [piece for piece in pieces if piece.start < half]
-    late = [piece for piece in pieces if piece.start >= half]
+    ahead = entries // 2
+    early_sums = [slice(start, start + PIECE) for start in range(0, ahead, PIECE)]
+    late_sums = [slice(start, start + PIECE) for start in range(ahead, entries, PIECE)]
+    starts = list(range(0, entries, PIECE)) + [entries - PIECE // 2]
+    gate_pieces = [slice(start, stop) for start, stop in zip(starts, starts[1:] + [entries])]
 
     with tc.tile_pool(name="held", bufs=1) as held:
         offsets = held.tile([rows, entries // ENTRIES_PER_COLUMN], U16, name="offsets")
@@ -38,24 +39,24 @@ def tile_lookup_vg_addsig_out_kernel(tc, tab, y, offs, out):
             nc.vector.tensor_tensor(product[:, piece], summed[:, piece], opened[:, piece], mybir.AluOpType.mult)
             nc.sync.dma_start(out[:, piece], product[:, piece])
 
-        nc.sync.dma_start(offsets[:], offs)
         nc.sync.dma_start(values[:], tab[0])
-        nc.sync.dma_start(stream[:, :half], y[:, :half])
+        nc.sync.dma_start(offsets[:], offs)
+        nc.sync.dma_start(stream[:, :ahead], y[:, :ahead])
         nc.sync.dma_start(gates[:], tab[1])
-        for piece in late:
+        for piece in late_sums:
             nc.sync.dma_start(stream[:, piece], y[:, piece])
 
         nc.vector.memset(warm_in[:], 0.0)
         nc.scalar.activation(warm_out[:], warm_in[:], mybir.ActivationFunctionType.Sigmoid)
 
-        for piece in early:
+        for piece in early_sums:
             add_values(piece)
-        for piece in pieces:
+        for piece in gate_pieces:
             nc.scalar.activation(
                 opened[:, piece], gates[:].indirect(listed(piece)), mybir.ActivationFunctionType.Sigmoid
             )
-        for early_piece, late_piece in zip(early, late):
-            add_values(late_piece)
-            multiply_and_store(early_piece)
-        for piece in late:
+        for sum_piece, gate_piece in zip(late_sums, gate_pieces):
+            add_values(sum_piece)
+            multiply_and_store(gate_piece)
+        for piece in gate_pieces[len(late_sums) :]:
             multiply_and_store(piece)

@@ -10,7 +10,7 @@ def tile_lookup_vg_addsig_out_kernel(tc, tab, y, offs, out):
     nc = tc.nc
     rows, places = tab.shape[1], tab.shape[2]
     entries = y.shape[1]
-    ahead = entries // 2
+    ahead = entries - PIECE
     early_sums = [slice(start, start + PIECE) for start in range(0, ahead, PIECE)]
     late_sums = [slice(start, start + PIECE) for start in range(ahead, entries, PIECE)]
     starts = list(range(0, entries, PIECE)) + [entries - PIECE // 2]

import concourse.mybir as mybir

F32 = mybir.dt.float32
U16 = mybir.dt.uint16
ENTRIES_PER_COLUMN = 16
PIECE = 256


def tile_lookup_vg_addsig_out_kernel(tc, tab, y, offs, out):
    nc = tc.nc
    rows, places = tab.shape[1], tab.shape[2]
    entries = y.shape[1]
    ahead = entries - PIECE
    early_sums = [slice(start, start + PIECE) for start in range(0, ahead, PIECE)]
    late_sums = [slice(start, start + PIECE) for start in range(ahead, entries, PIECE)]
    starts = list(range(0, entries, PIECE)) + [entries - PIECE // 2]
    gate_pieces = [slice(start, stop) for start, stop in zip(starts, starts[1:] + [entries])]

    with tc.tile_pool(name="held", bufs=1) as held:
        offsets = held.tile([rows, entries // ENTRIES_PER_COLUMN], U16, name="offsets")
        values = held.tile([rows, places], F32, name="values")
        gates = held.tile([rows, places], F32, name="gates")
        stream = held.tile([rows, entries], F32, name="stream")
        summed = held.tile([rows, entries], F32, name="summed")
        opened = held.tile([rows, entries], F32, name="opened")
        product = held.tile([rows, entries], F32, name="product")
        warm_in = held.tile([rows, 8], F32, name="warm_in")
        warm_out = held.tile([rows, 8], F32, name="warm_out")

        def listed(piece):
            return offsets[:, piece.start // ENTRIES_PER_COLUMN : piece.stop // ENTRIES_PER_COLUMN]

        def add_values(piece):
            nc.vector.tensor_tensor(
                summed[:, piece], values[:].indirect(listed(piece)), stream[:, piece], mybir.AluOpType.add
            )

        def multiply_and_store(piece):
            nc.vector.tensor_tensor(product[:, piece], summed[:, piece], opened[:, piece], mybir.AluOpType.mult)
            nc.sync.dma_start(out[:, piece], product[:, piece])

        nc.sync.dma_start(values[:], tab[0])
        nc.sync.dma_start(offsets[:], offs)
        nc.sync.dma_start(stream[:, :ahead], y[:, :ahead])
        nc.sync.dma_start(gates[:], tab[1])
        for piece in late_sums:
            nc.sync.dma_start(stream[:, piece], y[:, piece])

        nc.vector.memset(warm_in[:], 0.0)
        nc.scalar.activation(warm_out[:], warm_in[:], mybir.ActivationFunctionType.Sigmoid)

        for piece in early_sums:
            add_values(piece)
        for piece in gate_pieces:
            nc.scalar.activation(
                opened[:, piece], gates[:].indirect(listed(piece)), mybir.ActivationFunctionType.Sigmoid
            )
        for sum_piece, gate_piece in zip(late_sums, gate_pieces):
            add_values(sum_piece)
            multiply_and_store(gate_piece)
        for piece in gate_pieces[len(late_sums) :]:
            multiply_and_store(piece)
